import numpy as np, ml_dtypes
CORES = [78,86,94,102,110,118]
N = 6
BF = ml_dtypes.bfloat16
def gentries(a):
    return np.ascontiguousarray(a.reshape(8, 16, -1).transpose(0, 2, 1)).reshape(8, -1)
def gtable(e):
    e = np.asarray(e); return np.ascontiguousarray(e.reshape(8, -1, 16).transpose(0, 2, 1)).reshape(128, -1).astype(np.int32)
L, A, B, H, RO, K = 1536, 192, 2, 2, 2, 11
def woven(rng, lens, ring):
    lens = np.asarray(lens); e = np.add.accumulate(lens); s = e - lens; ring = np.asarray(ring) & (lens > 2)
    nx = np.arange(1, L + 1); nx[e - 1] = np.where(ring, s, L)
    pv = np.arange(-1, L - 1); pv[s] = np.where(ring, e - 1, L)
    p = np.append(rng.permutation(L), L); a = np.zeros((2, L), np.int64); a[0, p[:L]] = p[nx]; a[1, p[:L]] = p[pv]
    return np.where(rng.random(L) < 0.5, a[::-1], a), p[:L]
def hills(rng, lens, p):
    lens = np.asarray(lens); k = np.repeat(np.arange(len(lens)), lens); at = np.arange(L) - (np.add.accumulate(lens) - lens)[k]; sh = (len(lens), 16)
    top = rng.random(sh) * lens[:, None]; steep = np.minimum(np.exp2(1 + 5 * rng.random(sh)) * np.power(lens.astype(np.float64), -1.0)[:, None], 0.5); high = 0.3 + 0.7 * rng.random(sh)
    v = high[k] * np.maximum(np.exp(-np.abs(at[:, None] - top[k]) * steep[k]), 0.05) * (0.5 + 0.5 * rng.random((L, 16)))
    x = np.zeros((L, 16), np.int32); x[p] = np.floor(255 * v).astype(np.int32)
    return x
def cands(rng, a):
    free = (a[0] == L) | (a[1] == L); own = np.arange(L); c = np.zeros((B + H, L), np.int64)
    for i in range(B):
        o = np.argsort(rng.random(L) + np.where(free, 0.0, 1.0) * (rng.random(L) < 0.8)); c[i, o[0::2]] = o[1::2]; c[i, o[1::2]] = o[0::2]
        u = rng.random(L); w = a[rng.integers(0, 2, L), own]
        c[i] = np.where(u < 0.15, rng.integers(0, L, L), np.where((u < 0.3) & (w < L), w, np.where((u > 0.3) & (u < 0.32), own, c[i])))
    c[B:] = rng.integers(0, A, (H, L))
    return c
def cuts(rng, n, span):
    o = np.sort(rng.permutation(span - 1)[:n - 1]) + 1
    return np.diff(np.concatenate([[0], o, [L]]))
def ends(rng, n):
    if n < 2: return np.array([1] * n + [L - n]), np.array([False] * n + [True])
    one = n % 2; h = n // 2; rest = L - one - 2 * h; o = np.sort(rng.integers(0, rest + 1, h - 1))
    lens = np.concatenate([np.ones(one, np.int64), 2 + np.diff(np.concatenate([[0], o, [rest]]))])
    return lens, np.zeros(len(lens), bool)
def common(rng, q):
    n = (3, 12, 60, 150)[(q + q // 8) % 4]
    return cuts(rng, n, int(L * (0.3 + 0.6 * rng.random()))), rng.random(n) < 0.2
def parts(rng, form, bind=None):
    M, X, C = [], [], []
    for q in range(8 * N):
        lens, ring = form(rng, q); a, p = woven(rng, lens, ring); x = hills(rng, lens, p); c = cands(rng, a)
        if bind is not None: bind(q, lens, p, x, c)
        M.append(a); X.append(x); C.append(c)
    return np.stack(M), np.stack(X), np.stack(C)
def levels(rng, M, X, C, share, hold=False, bump=0, still=None, fix=None):
    th, left = [], []; still = np.zeros(8 * N, bool) if still is None else still; fix = np.full((8 * N, RO), -1) if fix is None else fix
    for t in range(RO):
        m, E, W = walks(M, X); v = np.sort(np.where(m < L, W, 0), axis=1); c = np.add.reduce((m < L).astype(np.int64), axis=1)
        i = np.clip(2 * L - 1 - np.floor(share * c).astype(np.int64), 0, 2 * L - 1)
        b = np.clip(v[np.arange(8 * N), i] + rng.integers(0, bump + 1, 8 * N), 1, 8160)
        if hold and t == 0: b = np.full(8 * N, 8192)
        b = np.where(still, 8192, b); b = np.where(fix[:, t] >= 0, fix[:, t], b); th.append(b)
        m = np.where((m < L) & (W >= b[:, None]), L, m); left.append(np.add.reduce(((m[:, :L] == L) | (m[:, L:] == L)).astype(np.int64), axis=1))
        if t < RO - 1: M, X = turn(C, X, E, m)
    assert np.all(left[-1][still] <= np.minimum(A, left[0][still]) * 3 // 4)
    return np.stack(th, axis=1)
def pack(M, X, C, th):
    return {"nb": np.stack([gtable(a) for a in M.reshape(N, 8, -1)]), "cd": np.stack([gtable(a) for a in C.reshape(N, 8, -1)]),
            "th": np.repeat(th, 16, axis=0).reshape(N, 128, RO).astype(np.int32), "x0": np.ascontiguousarray(X.transpose(0, 2, 1)).reshape(N, 128, L).astype(np.float32).astype(BF)}
def setup_inputs(rng):
    M, X, C = parts(rng, common)
    return pack(M, X, C, levels(rng, M, X, C, 0.02 + 0.28 * rng.random(8 * N)))
def setup_inputs_room(rng):
    q = np.arange(8 * N); still = (q % 8 == 1) | (q % 8 == 4) | (q % 8 == 6); fall = (q % 8 == 7) & (q // 8 % (H + 1) < H)
    size = np.where(still, np.array([A, A + 1, A // 2])[(q // 8 + q % 8) % 3], np.array([A, A + 1, A - 1, 0, 1, 2 * A, A, A + 1])[(q + q // 8) % 8])
    size = np.where(q % 8 == 7, np.where(fall, A - 16, 2 * A), size); fix = np.where((q % 8 == 7)[:, None], rng.integers(8161, 8193, (8 * N, RO)), -1)
    def bind(q, lens, p, x, c):
        e = np.add.accumulate(lens); s = e - lens
        if q % 8 == 7:
            u, w = p[e - 1], p[s]; x[w] = 255
            if fall[q]:
                f = np.roll(w, -1); x[u] = 255; c[:B, u] = f; c[:B, f] = u
                if q // 8 >= N // 2: c[:B, u[:4]] = u[:4]; c[:B, f[:4]] = f[:4]
            else:
                c[:B, u] = u; c[:B, w] = p[s + 1]; c[B:, u] = rng.integers(0, A - 16, (H, len(u))); c[B:, u[0]] = A - 17; c[B:, w] = rng.integers(A - 16, A, (H, len(w)))
            return
        if not still[q]: return
        k = np.nonzero(lens > 1)[0]; k = k[:len(k) // 2 * 2]
        i, j = k[0::2], k[1::2]; u, v, w = p[e[i] - 1], p[e[j] - 1], p[s[i]]
        big = np.maximum.reduceat(x[p], s, axis=0); x[u] = np.maximum(big[i], big[j]); x[v] = x[u]
        c[:B, u] = v; c[:B, v] = u; c[:B, w] = w
        for d in range(1, H + 1):
            top = min(A, int(size[(q - 8 * d) % (8 * N)])); c[B + d - 1, w] = rng.integers(top * 3 // 4, top, len(w)); c[B + d - 1, w[0]] = top - 1
    M, X, C = parts(rng, lambda rng, q: ends(rng, int(size[q])), bind)
    return pack(M, X, C, levels(rng, M, X, C, 0.02 + 0.28 * rng.random(8 * N), hold=True, still=still, fix=fix))
def setup_inputs_ties(rng):
    M, X, C = parts(rng, common); X = X // 64 * 85
    return pack(M, X, C, levels(rng, M, X, C, 0.02 + 0.28 * rng.random(8 * N), bump=1))
def setup_inputs_rings(rng):
    def form(rng, q):
        i = (q + q // 8) % 8; k = L // 3
        if i == 0: lens = [L]
        elif i == 1: lens = [1, L - 1]
        elif i == 2: lens = [L]
        elif i == 3: lens = [3] * k + [L - 3 * k] * int(L > 3 * k)
        elif i == 4: lens = [2] * (L // 2)
        elif i == 5: lens = cuts(rng, 40, L // 2)
        elif i == 6: lens = [1] * L
        else: lens = cuts(rng, 60, L // 2)
        return np.array(lens), (rng.random(len(lens)) < 0.5) if i == 7 else np.full(len(lens), i != 2)
    M, X, C = parts(rng, form); X = rng.integers(0, 16, (8 * N, L, 16)).astype(np.int32)
    X[np.arange(8 * N)[:, None], rng.integers(0, L, (8 * N, 16)), np.arange(16)] = rng.integers(100, 256, (8 * N, 16))
    fix = np.full((8 * N, RO), -1)
    for q in range(8 * N):
        i = (q + q // 8) % 8
        if q // 8 % 2 == 0 and i == 4:
            X[q] = np.where(np.arange(L) < np.minimum(M[q, 0], M[q, 1]), 255, 0)[:, None]; fix[q] = (8161, 8192)[q // 16 % 2]
        if q // 8 % 2 == 0 and i == 6:
            o = rng.permutation(L); u, v = o[0::2], o[1::2]; c = C[q]; c[:B, u] = v; c[:B, v] = v; c[B - 1, v] = u
            x = rng.integers(64, 256, (L, 16)); x[v] = x[u]; X[q] = x; fix[q] = 8192
    return pack(M, X, C, levels(rng, M, X, C, 0.02 + 0.28 * rng.random(8 * N), bump=1, fix=fix))
def setup_inputs_alike(rng):
    M, X, C = parts(rng, common); own = np.arange(L); fix = np.full((8 * N, RO), -1)
    for q in range(8 * N):
        g = q % 8
        if g < 2: C[q, :B] = rng.choice(np.array([0, L - 1, L // 2, 3]), (B, L))
        if g == 2: w = M[q][rng.integers(0, 2, (B, L)), own]; C[q, :B] = np.where(w < L, w, own)
        if g in (3, 4): C[q, 1:B] = C[q, 0]
        if g == 5: X[q] = 77
        if g == 5 and q // 8 % 2 == 0: fix[q, 0] = 0
        if g % 2 == 0: C[q, B:] = rng.choice(np.array([0, 1, A - 1]), (H, L))
    return pack(M, X, C, levels(rng, M, X, C, 0.02 + 0.28 * rng.random(8 * N), fix=fix))
def setup_inputs_spread(rng):
    M, X, C = parts(rng, common)
    v = 256 * rng.random((8 * N, L, 16)) * np.exp2(-rng.integers(0, 9, (8 * N, L, 1))) * (rng.random((8 * N, L, 1)) > 0.0625)
    X = np.minimum(np.floor(v), 255).astype(np.int32)
    return pack(M, X, C, levels(rng, M, X, C, rng.random(8 * N) ** 3))
def check_inputs(d):
    bad = []; G = np.arange(8 * N)[:, None]; own = np.arange(L)
    M = np.stack([gentries(a) for a in d["nb"]]).astype(np.int64).reshape(8 * N, 2, L); C = np.stack([gentries(a) for a in d["cd"]]).astype(np.int64).reshape(8 * N, B + H, L)
    if np.min(M) < 0 or np.max(M) > L: bad.append("range of nb")
    else:
        if np.any(M == own): bad.append("nb: a layer linked to itself")
        if np.any((M[:, 0] == M[:, 1]) & (M[:, 0] < L)): bad.append("nb: both slots name one layer")
        P = np.concatenate([M, np.full((8 * N, 2, 1), L)], axis=2)
        for s in range(2):
            m = M[:, s]
            if not np.all((m == L) | (P[:, 0][G, m] == own) | (P[:, 1][G, m] == own)): bad.append("nb: a link of one side only, slot " + str(s))
    if np.min(C) < 0 or np.max(C[:, :B]) > L - 1 or np.max(C[:, B:]) > A - 1: bad.append("range of cd")
    t = d["th"].reshape(8 * N, 16, RO)
    if np.min(t) < 0 or np.max(t) > 8192: bad.append("range of th")
    if np.any(t != t[:, :1]): bad.append("th: rows of a group that differ")
    v = d["x0"].astype(np.float32)
    if not np.all((v >= 0) & (v <= 255) & (v == np.floor(v))): bad.append("x0: whole numbers from 0 to 255")
    return bad
def walks(M, X):
    Q = len(M); G = np.arange(Q)[:, None]; m = M.reshape(Q, 2 * L)
    came = np.concatenate([M[:, 0], np.full((Q, 1), L)], axis=1)[G, m] == np.tile(np.arange(L), 2)
    back = np.where(m < L, np.where(came, m, L + m), 2 * L)
    step = np.concatenate([np.where(m < L, np.where(came, L + m, m), 2 * L), np.full((Q, 1), 2 * L)], axis=1)
    E = np.concatenate([X, X, np.zeros((Q, 1, 16), X.dtype)], axis=1); P = step[G, step]
    for k in range(K):
        E = np.maximum(E, E[G, P]); P = P[G, P]
    D = np.add.reduce(np.abs(E - E[G, step]), axis=2)
    return m, E, D[:, :2 * L] + D[G, back]
def turn(C, X, E, m):
    Q = len(X); G = np.arange(Q)[:, None]; own = np.arange(L); M = m.reshape(Q, 2, L)
    X = (X + np.abs(E[:, :L] - E[:, L:2 * L])) >> 1
    free = (M[:, 0] == L) | (M[:, 1] == L); place = np.add.accumulate(free.astype(np.int64), axis=1) - 1
    q, n = np.nonzero(free & (place < A)); S = np.zeros((Q, A, 16), X.dtype); S[q, place[q, n]] = X[q, n]
    S = S.reshape(N, 8, A, 16)
    come = [np.roll(S, d, axis=0).reshape(Q, A, 16)[G, C[:, B + d - 1]] for d in range(1, H + 1)]
    far = []
    for i in range(B):
        c = C[:, i]; ok = free[G, c] & (c != own) & (c != M[:, 0]) & (c != M[:, 1])
        far.append(np.where(ok, np.add.reduce(np.abs(X - X[G, c]), axis=2), 2 ** 20))
    for v in come: far.append(np.add.reduce(np.abs(X - v), axis=2))
    pick = np.argmin(np.stack(far, axis=1), axis=1)
    to = np.where(free & (pick < B), np.take_along_axis(C, pick[:, None, :], 1)[:, 0], L)
    both = (to < L) & (np.concatenate([to, np.full((Q, 1), L)], axis=1)[G, to] == own); low = M[:, 0] == L
    M = np.stack([np.where(both & low, to, M[:, 0]), np.where(both & ~low, to, M[:, 1])], axis=1)
    for d, v in enumerate(come): X = np.where((free & (pick == B + d))[:, :, None], (X + v) >> 1, X)
    return M, X
def reference(nb, cd, th, x0):
    M = np.stack([gentries(a) for a in nb]).astype(np.int64).reshape(8 * N, 2, L); C = np.stack([gentries(a) for a in cd]).astype(np.int64).reshape(8 * N, B + H, L)
    X = np.ascontiguousarray(x0.astype(np.float32).reshape(8 * N, 16, L).transpose(0, 2, 1)).astype(np.int32); t = th.astype(np.int64).reshape(8 * N, 16, RO)[:, 0]
    for rnd in range(RO):
        m, E, W = walks(M, X)
        M, X = turn(C, X, E, np.where((m < L) & (W >= t[:, rnd:rnd + 1]), L, m))
    return {"yn": np.stack([gtable(a) for a in M.reshape(N, 8, 2 * L)]).astype(np.float32), "yx": np.ascontiguousarray(X.transpose(0, 2, 1)).reshape(N, 128, L).astype(np.float32).astype(BF)}

from concourse.bass import DstId, RemoteDMATransfer
from concourse.mybir import AluOpType, ActivationFunctionType

L = 1536
S = 2 * L
A = 192
H = 2
RO = 2
K = 11
W = S + 16
AR = L + 16
HALF = L // 16
QUART = HALF // 2
MAGIC = 12582912.0
SHARE = {"t0": 48, "g1a": 42, "g1b": 42, "tsa": 30, "tsb": 48, "p0a": 48, "p0b": 48, "ba": 36, "bb": 48, "xf": 30,
         "tq": 24, "gq": 48, "vme": 32, "vm0": 48, "vm1": 48, "ts2a": 24, "ts2b": 32, "p2a": 48, "p2b": 40}

SCRATCH = {}
for _n, _c in (("nbi", 192), ("cdi", 384), ("thi", 2), ("pi", 1), ("pa", 1), ("pb", 1)):
    SCRATCH[_n] = ("sbuf", [128, _c], "int32")
for _n, _c in (("Lm", 192), ("Ls", 192), ("LP0", 192), ("LP1", 192), ("Lc", 384), ("Lb", 192), ("Lcnt", 12),
               ("Ln", 12), ("Lxf", 96), ("Lq", 96), ("Lto", 96), ("Lmix", 96)):
    SCRATCH[_n] = ("sbuf", [128, _c], "uint16")
for _n, _c in (("par", 1), ("ev", 1), ("pg", 1), ("wc", 1), ("g16", 8), ("hc", 13), ("hm", 13), ("sid", 192),
               ("kk", 192), ("kb", 12), ("thf", 2), ("M", 192), ("M2", 192), ("st", 192), ("t1", 192), ("t2", 192),
               ("e", 192), ("cf", 384), ("dc", 96), ("Rc", 96), ("da", 96), ("fs", 192), ("fs2", 192),
               ("base", 192), ("cum", 97), ("incl", 97), ("one", 96), ("junk", 96), ("acc", 12), ("u", 192),
               ("k0", 96), ("sel", 96), ("ko", 96), ("R", 96), ("Q", 96), ("f1", 96), ("low", 96), ("far2", 96),
               ("ka", 96), ("ow", 96), ("q", 96), ("a3", 96), ("mx", 96), ("zz", 96), ("d0", 96), ("d1", 96),
               ("tx", 96), ("big", 512), ("If", 128), ("nIf", 128)):
    SCRATCH[_n] = ("sbuf", [128, _c], "float32")
for _n, _c in (("i256", 256), ("ident", W), ("Zp", 144), ("Zs", 144), ("T0", AR), ("XX", W), ("EA", W), ("EB", W),
               ("EC", S), ("PA", W), ("PB", W), ("Dd", S), ("Aa", W), ("Bb", S), ("D2", S), ("B2", S), ("Gq", L),
               ("Fa", L), ("xf", L), ("vm", L), ("XW0", AR + H * A), ("XW1", AR + H * A), ("blk0", A), ("blk1", A),
               ("fm", 96), ("fl", A), ("cntb", 12), ("I05", 128), ("nI05", 128), ("I16", 128), ("Ibig", 128),
               ("Gall", 128), ("Tri", 128), ("g128", 128), ("mh", 128), ("on", 512), ("eu", 192), ("ew", 192),
               ("ex", 192), ("nfl", 96), ("nw", 96)):
    SCRATCH[_n] = ("sbuf", [128, _c], "bfloat16")
for _n in ("p0", "p1", "p2", "p3", "p4", "h0", "h1", "h2"):
    SCRATCH[_n] = ("psum", [128, 512], "float32")

SEMAPHORES = (["cv", "cs", "ct", "cg", "sent"] + ["arr%d%d" % (t, d) for t in range(RO) for d in range(H)]
              + ["dm%d" % i for i in range(16)] + ["tw%d" % i for i in range(4)])


def rank_program(g, core, T, topo):
    rank = T.rank_of(core)
    if rank is None:
        return
    n_ranks = len(T.cores)
    OP, AF = AluOpType, ActivationFunctionType
    queue = {"v": g.vector, "s": g.scalar, "t": g.tensor, "g": g, "y": g.sync}
    own_sem = {"v": "cv", "s": "cs", "t": "ct", "g": "cg"}
    count = {}
    seen = {q: {} for q in queue}
    known = {}
    hist = {}
    dmas = [0]

    def c(name, lo=0, hi=None, step=1):
        if hi is None:
            hi = SCRATCH[name][1][1]
        ap = T[name][:, lo:hi] if step == 1 else T[name][:, lo:hi:step]
        if SCRATCH[name][0] == "psum":
            return (ap, [(name, 0, 512)])
        return (ap, [(name, lo, hi)])

    def ind(win, off):
        return (win[0].indirect(off[0]), win[1] + off[1])

    def wait(q, sem, n):
        if seen[q].get(sem, 0) >= n:
            return
        queue[q].wait_ge(T.sem[sem], n)
        seen[q][sem] = n
        for s2, n2 in known.get((sem, n), {}).items():
            if seen[q].get(s2, 0) < n2:
                seen[q][s2] = n2

    def issue(q, emit, outs, ins, sem=None, inc=1):
        acc = [(r, True) for o in outs for r in o[1]] + [(r, False) for i in ins for r in i[1]]
        need = {}
        for (name, lo, hi), wr in acc:
            bank = SCRATCH[name][0] == "psum"
            for h in hist.get(name, []):
                if h[0] < hi and lo < h[1] and (wr or h[2] or (bank and h[5] != q)):
                    if q == "t" and h[5] == "t":
                        continue
                    need[h[3]] = max(need.get(h[3], 0), h[4])
        for s2 in sorted(need, key=lambda s3: s3 == own_sem.get(q)):
            wait(q, s2, need[s2])
        if sem is None:
            sem = own_sem[q]
        count[sem] = count.get(sem, 0) + inc
        emit().then_inc(T.sem[sem], inc)
        known[(sem, count[sem])] = dict(seen[q])
        for (name, lo, hi), wr in acc:
            old = hist.get(name, [])
            if wr:
                old = [h for h in old if not (lo <= h[0] and h[1] <= hi)]
            hist[name] = old + [[lo, hi, wr, sem, count[sem], q]]

    def col(x):
        return [x] if isinstance(x, tuple) else []

    def val(x):
        return x[0] if isinstance(x, tuple) else x

    def cp(o, i):
        issue("v", lambda: g.vector.tensor_copy(o[0], i[0]), [o], [i])

    def tt(o, a, b, op):
        issue("v", lambda: g.vector.tensor_tensor(o[0], a[0], b[0], op), [o], [a, b])

    def ts(o, a, s1, op0, s2=None, op1=None):
        if op1 is None:
            issue("v", lambda: g.vector.tensor_scalar(o[0], a[0], val(s1), None, op0), [o], [a] + col(s1))
        else:
            issue("v", lambda: g.vector.tensor_scalar(o[0], a[0], val(s1), val(s2), op0, op1), [o],
                  [a] + col(s1) + col(s2))

    def fill(o, x):
        issue("v", lambda: g.vector.memset(o[0], x), [o], [])

    def act(o, i, f, bias=0.0, scale=1.0, acc=None):
        if acc is None:
            issue("s", lambda: g.scalar.activation(o[0], i[0], f, bias=val(bias), scale=val(scale)), [o],
                  [i] + col(bias) + col(scale))
        else:
            issue("s", lambda: g.scalar.activation(o[0], i[0], f, bias=val(bias), scale=val(scale),
                                                   accum_out=acc[0]), [o, acc], [i] + col(bias) + col(scale))

    def mm(o, pairs, start=True, stop=True):
        def emit():
            last = None
            for j, (l, r) in enumerate(pairs):
                last = g.tensor.matmul(o[0], l[0], r[0], start and j == 0, stop and j == len(pairs) - 1)
            return last
        issue("t", emit, [o], [x for p in pairs for x in p])

    def lin(o, plus, minus):
        mm(o, [(c("If"), x) for x in plus] + [(c("nIf"), x) for x in minus])

    def iota(o, pattern, base, mult):
        if SCRATCH[o[1][0][0]][2] == "int32":
            issue("g", lambda: g.iota(o[0], pattern, base, mult), [o], [])
        else:
            issue("g", lambda: g.iota(o[0], pattern, base, mult, allow_small_or_imprecise_dtypes=True), [o], [])

    def select(o, i, pattern, op, base, mult):
        issue("g", lambda: g.affine_select(o[0], i[0], pattern, op, 0.0, base, mult), [o], [i])

    def diagonal(name, x):
        iota(c(name), [[0, 128]], x, 0)
        select(c(name), c(name), [[-1, 128]], OP.is_equal, 0, 1)

    def dma(o, i, sem=None):
        if sem is None:
            sem = "dm%d" % dmas[0]
            dmas[0] += 1
        issue("y", lambda: g.sync.dma_start(o[0], i[0]), [o], [i], sem, 16)

    def hbm(ap):
        return (ap, [])

    def listed(Z, src, c0, n):
        return [(c(Z, 15 - i, 143 - i), (T[src][:, 16 * c0 + i:16 * (c0 + n):16], [(src, 16 * c0, 16 * (c0 + n))]))
                for i in range(16)]

    def pick(q, out, win, lst, c0, c1):
        if c0 == c1:
            return
        o = c(out, 16 * c0, 16 * c1)
        i = ind(win, c(lst, c0, c1))
        if q == "v":
            cp(o, i)
        else:
            act(o, i, AF.Copy)

    def both(out, win, lst, r, share):
        mid = r[1] - SHARE[share]
        pick("s", out, win, lst, r[0], mid)
        pick("v", out, win, lst, mid, r[1])

    def third(name, j):
        return c(name, 512 * j, 512 * j + 512)

    def halve(a, b):
        for j in range(3):
            if a is not None:
                mm(c("h%d" % j), [(c("mh"), c("on")), (c("I05"), third(a, j))], True, False)
            if b is not None:
                mm(c("h%d" % j), [(c("I05"), third(b, j))], False, True)

    def rounded(out, j):
        ts(third(out, j), c("h%d" % j), MAGIC, OP.add, -MAGIC, OP.add)

    lo_, hi_ = (0, HALF), (HALF, 2 * HALF)
    halves = (("p0", lo_), ("p1", hi_))
    nid, nid2 = c("sid", *lo_), c("sid", *hi_)

    dma(c("nbi"), hbm(T.nb[:]))
    dma(c("cdi"), hbm(T.cd[:]))
    dma(c("thi"), hbm(T.th[:]))
    dma(c("XX", 0, L), hbm(T.x0[:]))
    dma(c("XX", L, S), hbm(T.x0[:]))
    dma(c("xf"), hbm(T.x0[:]))

    iota(c("pi"), [[1, 1]], 0, 1)
    iota(c("hc"), [[1, 13]], 0, 0)
    iota(c("i256"), [[1, 256]], 0, 0)
    iota(c("g16"), [[16, 8]], 0, 0)
    iota(c("sid"), [[L, 2], [16, HALF]], 0, 1)
    diagonal("nIf", -1)
    iota(c("g128"), [[16, 8], [0, 16]], 0, 0)
    for b in ("XX", "EA", "EB"):
        iota(c(b, S, W), [[0, 16]], 0, 0)
    fill(c("Zp"), 0.0)
    fill(c("Zs"), 0.0)
    ts(c("pa"), c("pi"), 1, OP.bitwise_and)
    ts(c("pb"), c("pi"), 112, OP.bitwise_and)
    cp(c("par"), c("pa"))
    ts(c("ev"), c("pa"), -1.0, OP.mult, 1.0, OP.add)
    cp(c("pg"), c("pb"))
    ts(c("hm"), c("hc"), c("par"), OP.mult)
    ts(c("wc"), c("pa"), 31.875, OP.mult, 0.125, OP.add)

    def ident_block(q, h):
        n = 256 if h < 12 else 16
        o, i = c("ident", 256 * h, 256 * h + n), c("i256", 0, n)
        if q == "v":
            ts(o, i, c("ev"), OP.mult, c("hm", h, h + 1), OP.add)
        else:
            act(o, i, AF.Identity, bias=c("hm", h, h + 1), scale=c("ev"))
    for h in (0, 1, 2, 3, 12):
        ident_block("v", h)
    for h in (4, 5, 6, 7, 8, 9):
        ident_block("s", h)
    ts(c("sid"), c("sid"), c("pg"), OP.subtract)
    ts(c("Zp", 15, 143, 16), c("g16"), c("pg"), OP.is_equal, c("wc"), OP.mult)
    ts(c("Zs", 15, 143, 16), c("g16"), c("pg"), OP.is_equal)
    cp(c("T0", L, AR), c("ident", S, W))
    for b in ("PA", "PB"):
        cp(c(b, S, W), c("ident", S, W))
    cp(c("Lm"), c("nbi"))
    cp(c("M"), c("nbi"))
    both("T0", c("ident", 0, L + 1), "Lm", lo_, "t0")
    act(c("t1"), c("M"), AF.Relu, bias=-float(S) * (L - 1), scale=float(S))
    for (p, r), sh in zip(halves, ("g1a", "g1b")):
        both("Dd", c("T0", 0, L + 1), "Lm", r, sh)
        mm(c(p, 0, HALF), [(c("nIf"), nid)] + listed("Zp", "Dd", r[0], HALF))
        if p == "p0":
            tt(c("t1"), c("t1"), c("M"), OP.max)
        else:
            cp(c("thf"), c("thi"))
            ts(c("Gall"), c("g128"), c("pg"), OP.is_equal, 1.0 / 512, OP.mult)
    for p, r in halves:
        ts(c("e", *r), c(p, 0, HALF), 0.0, OP.is_equal, float(L), OP.mult)
        tt(c("st", *r), c("e", *r), c("t1", *r), OP.add)
        cp(c("Ls", *r), c("st", *r))
        if p == "p0":
            ident_block("v", 10)
            ident_block("v", 11)
            cp(c("cf"), c("cdi"))

    iota(c("kk"), [[3, A]], 0, 0)
    iota(c("kb"), [[-16, 12]], 0, -1)
    diagonal("If", 1)
    diagonal("I16", 16)
    diagonal("Ibig", 16384)
    iota(c("one"), [[0, HALF]], 1, 0)
    iota(c("on"), [[0, 512]], 1, 0)
    iota(c("cum", 0, 1), [[0, 1]], 0, 0)
    iota(c("Aa", S, W), [[0, 16]], 1024, 0)
    for t in range(RO):
        iota(c("XW%d" % t, L, AR), [[0, 16]], 0, 0)
        iota(c("XW%d" % t, L, L + 1), [[0, 1]], -8192, 0)
    select(c("Tri"), c("Gall"), [[1, 128]], OP.is_ge, 0, -1)

    def constants_scalar():
        ops = []
        for d in range(H):
            r = (192 + HALF * d, 192 + HALF * (d + 1))
            ops.append(lambda r=r, d=d: act(c("cf", *r), c("cf", *r), AF.Identity, bias=float(AR + A * d)))
        ops.append(lambda: (act(c("Rc"), c("cf", *lo_), AF.Identity, bias=float(L), scale=-1.0),
                            lin(c("p4", 0, HALF), [c("cf", *hi_)], [c("cf", *lo_)]),
                            lin(c("h0", 0, HALF), [c("cf", 288, 384)], [c("cf", 192, 288)])))
        ops.append(lambda: (act(c("I05"), c("If"), AF.Identity, scale=0.5),
                            lin(c("h1", 0, HALF), [c("cf", *lo_)], [nid]),
                            lin(c("h2", 0, HALF), [c("cf", *hi_)], [nid])))
        ops.append(lambda: act(c("nI05"), c("If"), AF.Identity, scale=-0.5))
        ops.append(lambda: act(c("dc"), c("p4", 0, HALF), AF.Copy))
        ops.append(lambda: act(c("da"), c("h0", 0, HALF), AF.Copy))
        ops.append(lambda: act(c("u", *lo_), c("h1", 0, HALF), AF.Abs))
        ops.append(lambda: act(c("u", *hi_), c("h2", 0, HALF), AF.Abs))
        ops.append(lambda: act(c("mh"), c("If"), AF.Identity, bias=-0.25 / 128, scale=0.0))
        return ops

    def from_steps():
        return [lambda: act(c("t1"), c("st"), AF.Relu, bias=-float(L - 1)),
                lambda: act(c("t1"), c("t1"), AF.Sign),
                lambda: act(c("t1"), c("t1"), AF.Identity, scale=float(L)),
                lambda: (act(c("t2"), c("st"), AF.Relu, bias=-float(L) * (S - 1), scale=float(L)),
                         lin(c("p2", 0, 192), [c("st")], [c("t1")]),
                         lin(c("p3", 0, 192), [c("st"), c("t2")], [c("t1"), c("t1")])),
                lambda: None,
                lambda: act(c("M"), c("p2", 0, 192), AF.Copy),
                lambda: ts(c("Lb"), c("p3", 0, 192), float(L), OP.add)]

    dsts = [T.cores[(rank + d) % n_ranks] for d in range(1, H + 1)]
    near = topo.mates(topo.chip(core), topo.chip(T.cores[(rank - 1) % n_ranks]))
    order = (0, 1) if near else (1, 0)

    for t in range(RO):
        last = t == RO - 1
        XW, blk = "XW%d" % t, "blk%d" % t
        if t == 0:
            both("PB", c("ident", 0, S + 1), "Ls", lo_, "tsa")
            both("PB", c("ident", 0, S + 1), "Ls", hi_, "tsb")
        for (p, r), sh in zip(halves, ("p0a", "p0b") if t == 0 else ("p2a", "p2b")):
            both("PA", c("PB", 0, S + 1), "Ls", r, sh)
            mm(c(p, 0, HALF), listed("Zp", "PA", r[0], HALF))
        src = "XX"
        side = from_steps() + (constants_scalar() if t == 0 else [])
        for k in range(K):
            lst = "LP%d" % (min(k, K - 2) % 2)
            dst = "EA" if k % 2 == 0 else "EB"
            pin, pout = ("PA", "PB") if k % 2 == 0 else ("PB", "PA")
            for p, r in halves:
                if k < K - 1:
                    cp(c(lst, *r), c(p, 0, HALF))
                if k < K - 2:
                    pick("s", pout, c(pin, 0, S + 1), lst, *r)
                    mm(c(p, 0, HALF), listed("Zp", pout, r[0], HALF))
                    if side:
                        side.pop(0)()
                elif p == "p0":
                    n = QUART // 2
                    part = [(16 * (QUART + n * j), 16 * (QUART + n * (j + 1))) for j in range(2)]
                    bank = [c("h%d" % j, 0, 16 * n) for j in range(2)]
                    for j in range(2):
                        pick("s", "Gq", c(src, 0, S + 1), lst, QUART + n * j, QUART + n * (j + 1))
                        mm(bank[j], [(c("nI05"), c(src, *part[j])), (c("I05"), c("Gq", *part[j]))])
                    for j in range(2):
                        act(c("vm", *part[j]), bank[j], AF.Relu, scale=2.0)
                        mm(bank[j], [(c("I05"), c(src, *part[j])), (c("I05"), c("vm", *part[j]))])
                    for j in range(2):
                        act(c(dst, *part[j]), bank[j], AF.Identity, scale=2.0)
                        if k == K - 1:
                            act(c("EC", *part[j]), bank[j], AF.Identity, scale=2.0)
                for j in (0, 1) if p == "p1" or k < K - 2 else (0,):
                    a = r[0] + QUART * j
                    cols = (16 * a, 16 * (a + QUART))
                    if k == 0:
                        twin = c("xf", cols[0] % L, cols[0] % L + 16 * QUART)
                    else:
                        twin = c(dst if k == K - 1 else "EC", *cols)
                    tt(c(dst, *cols), ind(c(src, 0, S + 1), c(lst, a, a + QUART)), twin, OP.max)
                    by = {K - 3: "d-gg", K - 2: "----", K - 1: "g-dd"}.get(k, "dgdg")[a // QUART]
                    if by == "g":
                        select(c("EC", *cols), c(dst, *cols), [[0, 16 * QUART]], OP.is_ge, 0, 0)
                    if by == "d":
                        dma(c("EC", *cols), c(dst, *cols), sem="tw%d" % (a // QUART))
            src = dst
        E = src
        for j in range(3):
            mm(c("h%d" % j), [(c("I05"), third(E, j)), (c("nI05"), third(E, 3 + j))])
            act(third("Fa", j), c("h%d" % j), AF.Abs, scale=2.0)
        for j in range(4):
            cols = (16 * QUART * j, 16 * QUART * (j + 1))
            tt(c("Dd", *cols), ind(c(E, 0, S + 1), c("Ls", QUART * j, QUART * (j + 1))), c("EC", *cols), OP.subtract)
            act(c("Aa", *cols), c("Dd", *cols), AF.Abs)
            if j == 0:
                halve("XX", "Fa")
            if j == 1:
                mm(c("p0", 0, HALF), listed("Zs", "Aa", 0, HALF), True, False)
        mm(c("p1", 0, HALF), listed("Zs", "Aa", HALF, HALF), True, False)
        for j in range(3):
            rounded(XW, j)
        for (p, r), sh in zip(halves, ("ba", "bb")):
            both("Bb", c("Aa", 0, S + 1), "Lb", r, sh)
            mm(c(p, 0, HALF), listed("Zs", "Bb", r[0], HALF), False, True)
        if t == 0:
            cp(c("Lc"), c("cdi"))
            act(c("ew"), c("u"), AF.Relu, bias=1.0, scale=-1.0)
            act(c("kb"), c("kb"), AF.Identity, bias=c("pg"))
            act(c("incl", HALF, HALF + 1), c("kb", 0, 1), AF.Identity, scale=-1e6)
            act(c("kb"), c("kb"), AF.Identity, bias=-1.5, scale=3.0)
        for p, r in halves:
            ts(c("fs", *r), c(p, 0, HALF), c("thf", t, t + 1), OP.is_ge, float(L), OP.mult)
        tt(c("fm"), c("fs", *lo_), c("fs", *hi_), OP.max)
        mm(c("p2", 0, HALF), [(c("Gall"), c("fm"))])
        mm(c("p3", 0, HALF), [(c("Tri"), c("fm"))])
        tt(c("tx"), nid2, c("fm"), OP.subtract)
        issue("v", lambda: g.vector.tensor_tensor_scan(T.cum[:, 1:HALF + 1], T.one[:], T.p2[:, 0:HALF], 0.0,
                                                       OP.mult, OP.add),
              [c("cum", 1, HALF + 1)], [c("one"), c("p2")])
        for j in range(12):
            act(c("junk"), c("cum", 1, HALF + 1), AF.Sign, bias=c("kb", j, j + 1), acc=c("acc", j, j + 1))
        ts(c("Lxf"), c("tx"), float(L), OP.min)
        tt(c("incl", 0, HALF), c("p3", 0, HALF), c("cum", 0, HALF), OP.add)
        tt(c("M2"), c("M"), c("fs"), OP.max)
        tt(c("eu"), c("cf", 0, 192), c("M2"), OP.is_equal)
        tt(c("ex", *lo_), c("cf", *lo_), c("M2", *hi_), OP.is_equal)
        tt(c("ex", *hi_), c("cf", *hi_), c("M2", *lo_), OP.is_equal)
        ts(c("Lcnt"), c("acc"), -0.5, OP.mult, HALF / 2.0, OP.add)
        act(c("cntb"), c("acc"), AF.Identity, bias=HALF / 2.0, scale=-0.5)
        tt(c("fl"), ind(c("incl"), c("Lcnt")), c("kk"), OP.is_le)
        mm(c("p4", 0, 12), listed("Zs", "fl", 0, 12) + [(c("I16"), c("cntb"))])
        both("xf", c(XW, 0, L + 1), "Lxf", lo_, "xf")
        cp(c("Ln"), c("p4", 0, 12))
        cp(c(blk), ind(c(XW, 0, L + 2), c("Ln")))
        transfers, share = [], None
        for d, dst in enumerate(dsts):
            eng = topo.engines(core, dst)
            share = len(eng) // H
            mask = 0
            for e in eng[d * share:(d + 1) * share]:
                mask |= 1 << e
            rid, pid, _ = topo.addr(dst)
            transfers.append(RemoteDMATransfer(dst_ids=[DstId(rid=rid, pnc=pid)], dma_engine_mask=mask,
                                               remote_sem=T.sem["arr%d%d" % (t, d)], src=T[blk][:],
                                               dst=T[XW][:, AR + A * d:AR + A * (d + 1)]))
        h = hist[blk][-1]
        wait("g", h[3], h[4])
        g.remote_dma_fused(transfers, local_sem=T.sem.sent)
        count["sent"] = count.get("sent", 0) + share * H
        for d in range(H):
            count["arr%d%d" % (t, d)] = share
            hist[XW].append([AR + A * d, AR + A * (d + 1), True, "arr%d%d" % (t, d), share, "remote"])
        act(c("nfl"), c("fm"), AF.Identity, bias=float(L), scale=-1.0)
        act(c("f1"), c("fm"), AF.Sign)
        act(c("low"), c("fs", *lo_), AF.Sign)
        if not last:
            act(c("fs2"), c("fs"), AF.Identity, scale=2.0)
        pick("s", "Dd", c("xf"), "Lc", 64, HALF)
        mm(c("h2"), [(c("nI05"), third(XW, 2)), (c("I05"), third("Dd", 2))])
        for p, r, end in (("p0", lo_, 64), ("p1", hi_, 2 * HALF)):
            cols = (16 * r[0], 16 * end)
            tt(c("Dd", *cols), ind(c("xf"), c("Lc", r[0], end)), c(XW, 0, cols[1] - cols[0]), OP.subtract)
            if p == "p0":
                act(third("Bb", 2), c("h2"), AF.Abs, scale=2.0)
            act(c("Bb", *cols), c("Dd", *cols), AF.Abs)
            mm(c(p, 0, HALF), [(c("Ibig"), c(x, *r)) for x in ("eu", "ex", "ew")] + [(c("I16"), c("nfl"))]
               + listed("Zs", "Bb", r[0], HALF))
        act(c("k0"), c("p0", 0, HALF), AF.Copy)
        for j in range(6):
            d = order[j // 3]
            at = 192 + HALF * d + 32 * (j % 3)
            tt(third("D2", j), ind(c(XW, AR + A * d, AR + A * (d + 1)), c("Lc", at, at + 32)), third(XW, j % 3),
               OP.subtract)
            if j == 5:
                act(c("far2"), c("p2", 0, HALF), AF.Copy)
            act(third("B2", j), third("D2", j), AF.Abs)
            if j == 2:
                mm(c("p2", 0, HALF), listed("Zs", "B2", 0, HALF))
            if j == 4:
                mm(c("p3", 0, 64), listed("Zs", "B2", HALF, 64))
        mm(c("p3", 64, HALF), listed("Zs", "B2", HALF + 64, 32))
        halve(XW, None)
        tt(c("sel"), c("p1", 0, HALF), c("k0"), OP.is_lt)
        tt(c("ko"), c("p1", 0, HALF), c("k0"), OP.min)
        tt(c("sel"), c("sel"), c("dc"), OP.mult)
        tt(c("R"), c("Rc"), c("sel"), OP.subtract)
        tt(c("Q"), c("R"), c("fs", *lo_), OP.add)
        ts(c("Lto"), c("R"), -1.0, OP.mult, float(L), OP.add)
        if not last:
            tt(c("base"), c("st"), c("fs2"), OP.max)
        tt(c("ka"), c("p3", 0, HALF), c("far2"), OP.min)
        tt(c("ow"), c("ko"), c("ka"), OP.is_le)
        tt(c("q"), c("ow"), c("Q"), OP.mult)
        ts(c("Lq"), c("q"), -1.0, OP.mult, float(S), OP.add)
        mid = HALF - SHARE["tq"]
        pick("s", "T0", c("ident", 0, S + 1), "Lq", 0, mid)
        tt(c("a3"), c("p3", 0, HALF), c("far2"), OP.is_lt if order[0] == 0 else OP.is_gt)
        tt(c("mx"), c("f1"), c("ow"), OP.subtract)
        tt(c("a3"), c("a3"), c("da"), OP.mult)
        tt(c("a3"), c("a3"), c("cf", 192, 288), OP.add)
        tt(c("a3"), c("a3"), c("mx"), OP.mult)
        tt(c("a3"), c("a3"), nid, OP.max)
        cp(c("Lmix"), c("a3"))
        pick("v", "T0", c("ident", 0, S + 1), "Lq", mid, HALF)
        act(c("nw"), c("ow"), AF.Identity, bias=1.0, scale=-1.0)
        both("Gq", c("T0", 0, L), "Lto", lo_, "gq")
        mm(c("p4", 0, HALF), [(c("nIf"), nid), (c("Ibig"), c("nw"))] + listed("Zp", "Gq", 0, HALF))
        early, mid = SHARE["vme"], HALF - SHARE["vm%d" % t]
        pick("s", "vm", c(XW), "Lmix", 0, early)
        pick("v", "vm", c(XW), "Lmix", mid, HALF)
        act(c("zz"), c("p4", 0, HALF), AF.Abs, bias=-L / 2.0)
        pick("s", "vm", c(XW), "Lmix", early, mid)
        halve(None, "vm")
        if last:
            tt(c("d0"), c("R"), c("low"), OP.mult)
            tt(c("d1"), c("R"), c("d0"), OP.subtract)
            ts(c("zz"), c("zz"), L / 2.0, OP.is_equal)
            for x, r in (("d0", lo_), ("d1", hi_)):
                tt(c(x), c(x), c("zz"), OP.mult)
                tt(c("u", *r), c("M2", *r), c(x), OP.subtract)
            dma(hbm(T.yn[:]), c("u"))
            act(c("big"), c("h2"), AF.Identity, bias=MAGIC)
            act(third("xf", 2), c("big"), AF.Identity, bias=-MAGIC)
            for j in range(3):
                if j < 2:
                    rounded("xf", j)
                dma(hbm(T.yx[:, 512 * j:512 * j + 512]), third("xf", j))
        else:
            tt(c("d0"), c("p4", 0, HALF), c("R"), OP.add)
            ts(c("zz"), c("zz"), L / 2.0, OP.is_equal)
            tt(c("d0"), c("d0"), c("zz"), OP.mult)
            tt(c("d1"), c("d0"), c("low"), OP.mult)
            tt(c("st", *lo_), c("base", *lo_), c("d1"), OP.subtract)
            cp(c("Ls", *lo_), c("st", *lo_))
            tt(c("d0"), c("d0"), c("d1"), OP.subtract)
            tt(c("st", *hi_), c("base", *hi_), c("d0"), OP.subtract)
            cp(c("Ls", *hi_), c("st", *hi_))
            both("PB", c("ident", 0, S + 1), "Ls", lo_, "ts2a")
            for j in range(3):
                rounded("XX", j)
                dma(third("xf", j), third("XX", j))
                dma(third("XX", 3 + j), third("XX", j))
            both("PB", c("ident", 0, S + 1), "Ls", hi_, "ts2b")

    for sem in sorted(count):
        wait("g", sem, count[sem])
